import numpy as np
import ml_dtypes


def mxq(x, axis, fmt="e4m3"):
    dtype, down = {"e4m3": (ml_dtypes.float8_e4m3fn, 7), "e5m2": (ml_dtypes.float8_e5m2, 14)}[fmt]
    v = np.moveaxis(np.asarray(x, np.float32).astype(ml_dtypes.bfloat16).astype(np.float64), axis, -1)
    blocks = v.reshape(v.shape[:-1] + (-1, 32))
    amax = np.abs(blocks).max(-1, keepdims=True)
    byte = np.maximum(np.where(amax > 0, np.frexp(amax)[1] - 1 + 127, 0) - down, 1)
    scale = np.exp2(byte - 127.0)
    codes = (blocks / scale).astype(np.float32).astype(dtype).astype(np.float64)
    return np.moveaxis((codes * scale).reshape(v.shape), -1, axis)


WIDE = False


def mx_kscale(k):
    if not WIDE:
        return np.ones(k)
    levels = np.array([10, -10, 5, -5, 0])
    if k % 512:
        return np.exp2(np.random.permutation(np.resize(levels, k // 32))).repeat(32)
    a = np.empty((k // 512, 16))
    for p in range(k // 512):
        a[p, :8] = np.random.permutation(np.resize(levels, 8))
        for g in range(8):
            far = levels[np.abs(levels - a[p, g]) >= 10]
            a[p, g + 8] = far[np.random.randint(len(far))]
    return np.exp2(a.ravel()).repeat(32)


def f64(x):
    return np.asarray(x).astype(np.float64)


def striped8(idx):
    return np.asarray(idx).reshape(8, -1, 16).transpose(0, 2, 1).reshape(128, -1).astype(np.uint16)


def unstriped8(offs):
    return offs.reshape(8, 16, -1).transpose(0, 2, 1).reshape(8, -1).astype(np.int64)


def pick8(x, idx, run):
    r = np.arange(len(x))
    return x[r[:, None], idx[r % (8 * run) // run]]


E2M1 = np.array([0.0, 0.5, 1.0, 1.5, 2.0, 3.0, 4.0, 6.0, -0.0, -0.5, -1.0, -1.5, -2.0, -3.0, -4.0, -6.0])


def pack_weight(w, fmt):
    k, n = w.shape
    w = f64(np.asarray(w, np.float32).astype(ml_dtypes.bfloat16)).reshape(k // 32, 32, n)
    amax = np.abs(w).max(1)
    if fmt == "e4m3":
        byte = np.frexp(amax)[1] - 1 + 127 - 7
    else:
        mant, ex = np.frexp(amax / 6.0)
        byte = np.where(mant > 0.5, ex, ex - 1) + 127
    byte = np.clip(np.where(amax > 0, byte, 1), 1, 254)
    scaled = (w * np.exp2(127.0 - byte)[:, None, :]).reshape(k, n).astype(np.float32)
    by_word = np.ascontiguousarray(scaled.reshape(k // 512, 128, 4, n).transpose(0, 1, 3, 2))
    if fmt == "e4m3":
        words = by_word.astype(ml_dtypes.float8_e4m3fn).view(np.uint8)
    else:
        c = by_word.astype(ml_dtypes.float4_e2m1fn).view(np.uint8) & 0xF
        words = (c[..., 0::2] | (c[..., 1::2] << 4)).reshape(k // 512, 128, 2 * n)
    return np.ascontiguousarray(words), np.ascontiguousarray(byte.astype(np.uint8).reshape(k // 512, 16, n))


def unpack_weight(words, scales, fmt):
    g, _, n = scales.shape
    words = np.ascontiguousarray(words).reshape(g, 128, n, -1)
    if fmt == "e4m3":
        vals = words.view(ml_dtypes.float8_e4m3fn).astype(np.float64)
    else:
        nib = np.empty((g, 128, n, 4), np.uint8)
        nib[..., 0::2] = words & 0xF
        nib[..., 1::2] = words >> 4
        vals = E2M1[nib]
    vals = vals * np.repeat(np.exp2(scales.astype(np.float64) - 127.0), 8, axis=1)[..., None]
    return vals.transpose(0, 1, 3, 2).reshape(g * 512, n)


def sigmoid(v):
    return 1.0 / (1.0 + np.exp(-v))


D, T, U, X, S, I, Q = 512, 1024, 1024, 1024, 1024, 512, 128


def setup_inputs():
    n = np.random.standard_normal
    idx = np.stack([np.random.permutation(T)[:I] for _ in range(8)])
    idx2 = np.stack([np.random.permutation(U)[:I] for _ in range(8)])
    idx3 = np.stack([np.random.permutation(X)[:I] for _ in range(8)])
    idx4 = np.stack([np.random.permutation(S)[:I] for _ in range(8)])
    idx5 = np.stack([np.random.permutation(U)[:I] for _ in range(8)])
    idx6 = np.stack([np.random.permutation(U)[:I] for _ in range(8)])
    fd = mx_kscale(D)
    keysp = pack_weight(n((D, T)) / fd[:, None], "e4m3")
    notesp = pack_weight(n((D, U)) / fd[:, None], "e2m1")
    usersp = pack_weight(n((D, X)) / fd[:, None], "e4m3")
    shelvesp = pack_weight(n((D, S)) / fd[:, None], "e2m1")
    return {
        "query": (n((D, Q)) * 1.0 / np.sqrt(D) * fd[:, None]).astype(np.float32),
        "keys_words": keysp[0],
        "keys_scales": keysp[1],
        "notes_words": notesp[0],
        "notes_scales": notesp[1],
        "users_words": usersp[0],
        "users_scales": usersp[1],
        "shelves_words": shelvesp[0],
        "shelves_scales": shelvesp[1],
        "thr": (np.random.uniform(-0.6, 0.6, (Q, 1))).astype(np.float32),
        "slope": (np.random.uniform(1.0, 3.0, (Q, 1))).astype(np.float32),
        "offs": striped8(idx),
        "offs2": striped8(idx2),
        "offs3": striped8(idx3),
        "offs4": striped8(idx4),
        "offs5": striped8(idx5),
        "offs6": striped8(idx6),
    }


def reference(query, keys_words, keys_scales, notes_words, notes_scales, users_words, users_scales, shelves_words, shelves_scales, thr, slope, offs, offs2, offs3, offs4, offs5, offs6):
    idx = unstriped8(offs)
    idx2 = unstriped8(offs2)
    idx3 = unstriped8(offs3)
    idx4 = unstriped8(offs4)
    idx5 = unstriped8(offs5)
    idx6 = unstriped8(offs6)
    keysu = unpack_weight(keys_words, keys_scales, "e4m3")
    notesu = unpack_weight(notes_words, notes_scales, "e2m1")
    usersu = unpack_weight(users_words, users_scales, "e4m3")
    shelvesu = unpack_weight(shelves_words, shelves_scales, "e2m1")
    queryq = mxq(f64(query), 0, "e4m3")
    a = queryq.T @ keysu
    b = queryq.T @ notesu
    c0 = queryq.T @ usersu
    d0 = queryq.T @ shelvesu
    s1 = sigmoid(pick8(a, idx, 16) * f64(slope) + f64(thr))
    s2 = sigmoid(pick8(c0, idx3, 16) * f64(slope) + f64(thr))
    w = pick8(b, idx2, 16) * s1
    v = pick8(d0, idx4, 16) * s2
    r = w - v
    f1 = np.zeros((Q, U))
    f1[np.arange(Q)[:, None], idx5[np.arange(Q) % 128 // 16]] = r
    bb = b + f1
    y = pick8(bb, idx6, 16)
    return y

@@ -1,0 +1,192 @@
+from contextlib import ExitStack
+
+import concourse.mybir as mybir
+
+F32 = mybir.dt.float32
+BF16 = mybir.dt.bfloat16
+I32 = mybir.dt.int32
+U32 = mybir.dt.uint32
+U16 = mybir.dt.uint16
+U8 = mybir.dt.uint8
+FP8X4 = mybir.dt.float8_e4m3fn_x4
+FP4X4 = mybir.dt.float4_e2m1fn_x4
+MULT = mybir.AluOpType.mult
+ADD = mybir.AluOpType.add
+SIGMOID = mybir.ActivationFunctionType.Sigmoid
+COPY = mybir.ActivationFunctionType.Copy
+
+P = 128
+PACK = 4
+COLS = 1024
+BANK = 512
+SLOTS = 512
+HALF = SLOTS // 2
+GROUP = 16
+
+FLOPS = 2 * 512 * 128 * 4 * 1024
+
+
+def tile_attend_twolocks_four_kernel(
+    tc, query, keys_words, keys_scales, notes_words, notes_scales, users_words, users_scales,
+    shelves_words, shelves_scales, thr, slope, offs, offs2, offs3, offs4, offs5, offs6, out,
+):
+    nc = tc.nc
+    with ExitStack() as ctx:
+        sb = ctx.enter_context(tc.tile_pool(name="sb", bufs=1))
+        ps = ctx.enter_context(tc.psum_pool(name="ps", bufs=1))
+
+        def plane(name, engine):
+            t = sb.tile([P, COLS], U8, name=name, align_bytes=64)
+            engine.memset(t[:].bitcast(I32), 0)
+            return t
+
+        def load_rows(t, scales, r, queue):
+            rows = scales[0].bitcast(I32)
+            queue.dma_start(out=t[r:P:32, :].bitcast(I32), in_=rows[r:16:4, :])
+
+        def load_plane(t, scales, queues):
+            for r in range(4):
+                load_rows(t, scales, r, queues[r])
+
+        def load_list(name, src):
+            t = sb.tile([P, SLOTS // GROUP], U16, name=name)
+            nc.sync.dma_start(t[:], src)
+            return t
+
+        def load_fp8(name, words, queue):
+            t = sb.tile([P, COLS], U32, name=name, align_bytes=64)
+            queue.dma_start(out=t[:].bitcast(I32), in_=words[0].rearrange("p n t -> p (n t)").bitcast(I32))
+            return t
+
+        def load_fp4(name, words, queue):
+            t = sb.tile([P, 2 * COLS], U8, name=name, align_bytes=64)
+            queue.dma_start(out=t[:].bitcast(I32), in_=words[0].bitcast(I32))
+            return t
+
+        def load_col(name, src, queue):
+            t = sb.tile([P, 1], F32, name=name)
+            queue.dma_start(out=t[:], in_=src)
+            return t
+
+        users_plane = plane("users_plane", nc.gpsimd)
+        notes_plane = plane("notes_plane", nc.gpsimd)
+        shelves_plane = plane("shelves_plane", nc.vector)
+        keys_plane = plane("keys_plane", nc.vector)
+
+        q_raw = sb.tile([P, PACK, P], F32, name="q_raw")
+        nc.scalar.dma_start(out=q_raw[:], in_=query.rearrange("(p j) q -> p j q", j=PACK))
+        l3 = load_list("l3", offs3)
+        load_plane(users_plane, users_scales, [nc.scalar, nc.sync, nc.scalar, nc.sync])
+        load_plane(notes_plane, notes_scales, [nc.gpsimd] * 4)
+        users_w = load_fp8("users_w", users_words, nc.scalar)
+        thr_t = load_col("thr_t", thr, nc.sync)
+        shelves_w = load_fp4("shelves_w", shelves_words, nc.scalar)
+        load_plane(shelves_plane, shelves_scales, [nc.sync, nc.scalar, nc.sync, nc.scalar])
+        slope_t = load_col("slope_t", slope, nc.sync)
+        load_rows(keys_plane, keys_scales, 0, nc.scalar)
+        keys_w = load_fp8("keys_w", keys_words, nc.sync)
+        for r in range(1, 4):
+            load_rows(keys_plane, keys_scales, r, nc.sync)
+        l4 = load_list("l4", offs4)
+        notes_w = load_fp4("notes_w", notes_words, nc.sync)
+        l1 = load_list("l1", offs)
+        l2 = load_list("l2", offs2)
+        l5 = load_list("l5", offs5)
+        l6 = load_list("l6", offs6)
+
+        q_bf = sb.tile([P, P, PACK], BF16, name="q_bf", align_bytes=64)
+        nc.vector.tensor_copy(
+            out=q_bf[:].rearrange("p (c i) t -> p c t i", i=4),
+            in_=q_raw[:].rearrange("p t (c i) -> p c t i", i=4),
+        )
+        q_codes = sb.tile([P, P], U32, name="q_codes", align_bytes=64)
+        q_plane = sb.tile([P, P], U8, name="q_plane", align_bytes=64)
+        nc.vector.quantize_mx(
+            out=q_codes[:].bitcast(FP8X4), scales=q_plane[:], in_=q_bf[:].rearrange("p c t -> p (c t)")
+        )
+        f1 = sb.tile([P, COLS], F32, name="f1")
+        nc.vector.memset(f1[:], 0.0)
+
+        def scores(name, moving, scale_plane):
+            banks = []
+            for h in range(2):
+                bank = ps.tile([P, BANK], F32, name="%s_bank%d" % (name, h))
+                nc.tensor.matmul_mx(
+                    out=bank[:], lhsT=q_codes[:].bitcast(FP8X4), lhsT_scale=q_plane[:],
+                    rhs=moving[h], rhs_scale=scale_plane[:, h * BANK:(h + 1) * BANK], start=True, stop=True,
+                )
+                banks.append(bank)
+            return banks
+
+        def fp4_halves(t):
+            return [t[:, h * 2 * BANK:(h + 1) * 2 * BANK].bitcast(FP4X4) for h in range(2)]
+
+        def fp8_halves(t):
+            return [t[:, h * BANK:(h + 1) * BANK].bitcast(FP8X4) for h in range(2)]
+
+        c_ps = scores("c", fp8_halves(users_w), users_plane)
+        d_ps = scores("d", fp4_halves(shelves_w), shelves_plane)
+        a_ps = scores("a", fp8_halves(keys_w), keys_plane)
+        b_ps = scores("b", fp4_halves(notes_w), notes_plane)
+
+        a_sb = sb.tile([P, COLS], F32, name="a_sb")
+        b_sb = sb.tile([P, COLS], F32, name="b_sb")
+        c_sb = sb.tile([P, COLS], F32, name="c_sb")
+        d_sb = sb.tile([P, COLS], F32, name="d_sb")
+
+        def cols(h):
+            return slice(h * BANK, (h + 1) * BANK)
+
+        def part(lst, h):
+            return lst[:, h * (HALF // GROUP):(h + 1) * (HALF // GROUP)]
+
+        def new(name, h):
+            return sb.tile([P, HALF], F32, name="%s%d" % (name, h))
+
+        def gate(name, window, lst, h):
+            t = new(name, h)
+            nc.scalar.activation(t[:], window[:].indirect(part(lst, h)), SIGMOID, bias=thr_t[:], scale=slope_t[:])
+            return t
+
+        def fetch(name, window, lst, h):
+            t = new(name, h)
+            nc.scalar.activation(t[:], window[:].indirect(part(lst, h)), COPY)
+            return t
+
+        def neg_product(g, s, h):
+            t = new("nv", h)
+            nc.vector.scalar_tensor_tensor(t[:], g[:], -1.0, s[:], MULT, MULT)
+            return t
+
+        nc.vector.tensor_copy(out=c_sb[:, cols(0)], in_=c_ps[0][:])
+        nc.vector.tensor_copy(out=c_sb[:, cols(1)], in_=c_ps[1][:])
+        s2_0 = gate("s2_", c_sb, l3, 0)
+        nc.vector.tensor_copy(out=d_sb[:, cols(0)], in_=d_ps[0][:])
+        nc.vector.tensor_copy(out=d_sb[:, cols(1)], in_=d_ps[1][:])
+        g4_0 = fetch("g4_", d_sb, l4, 0)
+        nc.vector.tensor_copy(out=a_sb[:, cols(0)], in_=a_ps[0][:])
+        nc.scalar.copy(out=a_sb[:, cols(1)], in_=a_ps[1][:])
+        s1_0 = gate("s1_", a_sb, l1, 0)
+        nv_0 = neg_product(g4_0, s2_0, 0)
+        nc.vector.tensor_copy(out=b_sb[:, cols(0)], in_=b_ps[0][:])
+        nc.vector.tensor_copy(out=b_sb[:, cols(1)], in_=b_ps[1][:])
+        w_0 = new("w", 0)
+        nc.vector.tensor_tensor(w_0[:], b_sb[:].indirect(part(l2, 0)), s1_0[:], MULT)
+        nc.vector.tensor_tensor(f1[:].indirect(part(l5, 0)), w_0[:], nv_0[:], ADD)
+
+        s2_1 = gate("s2_", c_sb, l3, 1)
+        g4_1 = fetch("g4_", d_sb, l4, 1)
+        s1_1 = gate("s1_", a_sb, l1, 1)
+        g2_1 = fetch("g2_", b_sb, l2, 1)
+        nv_1 = neg_product(g4_1, s2_1, 1)
+        w_1 = new("w", 1)
+        nc.vector.tensor_tensor(w_1[:], g2_1[:], s1_1[:], MULT)
+        nc.vector.tensor_tensor(f1[:].indirect(part(l5, 1)), w_1[:], nv_1[:], ADD)
+
+        bb = sb.tile([P, COLS], F32, name="bb")
+        nc.vector.tensor_tensor(bb[:], b_sb[:], f1[:], ADD)
+        y_0 = new("y", 0)
+        nc.vector.tensor_copy(y_0[:], bb[:].indirect(part(l6, 0)))
+        nc.sync.dma_start(out=out[:, 0:HALF], in_=y_0[:])
+        y_1 = fetch("y", bb, l6, 1)
+        nc.scalar.dma_start(out=out[:, HALF:SLOTS], in_=y_1[:])

@@ -22,6 +22,7 @@ BANK = 512
 SLOTS = 512
 HALF = SLOTS // 2
 GROUP = 16
+SPLIT = 720
 
 FLOPS = 2 * 512 * 128 * 4 * 1024
 
@@ -35,9 +36,9 @@ def tile_attend_twolocks_four_kernel(
         sb = ctx.enter_context(tc.tile_pool(name="sb", bufs=1))
         ps = ctx.enter_context(tc.psum_pool(name="ps", bufs=1))
 
-        def plane(name, engine):
+        def plane(name):
             t = sb.tile([P, COLS], U8, name=name, align_bytes=64)
-            engine.memset(t[:].bitcast(I32), 0)
+            nc.vector.memset(t[:].bitcast(I32), 0)
             return t
 
         def load_rows(t, scales, r, queue):
@@ -68,30 +69,31 @@ def tile_attend_twolocks_four_kernel(
             queue.dma_start(out=t[:], in_=src)
             return t
 
-        users_plane = plane("users_plane", nc.gpsimd)
-        notes_plane = plane("notes_plane", nc.gpsimd)
-        shelves_plane = plane("shelves_plane", nc.vector)
-        keys_plane = plane("keys_plane", nc.vector)
+        users_plane = plane("users_plane")
+        keys_plane = plane("keys_plane")
+        shelves_plane = plane("shelves_plane")
+        notes_plane = plane("notes_plane")
 
         q_raw = sb.tile([P, PACK, P], F32, name="q_raw")
         nc.scalar.dma_start(out=q_raw[:], in_=query.rearrange("(p j) q -> p j q", j=PACK))
         l3 = load_list("l3", offs3)
-        load_plane(users_plane, users_scales, [nc.scalar, nc.sync, nc.scalar, nc.sync])
-        load_plane(notes_plane, notes_scales, [nc.gpsimd] * 4)
-        users_w = load_fp8("users_w", users_words, nc.scalar)
+        slope_t = load_col("slope_t", slope, nc.gpsimd)
         thr_t = load_col("thr_t", thr, nc.sync)
-        shelves_w = load_fp4("shelves_w", shelves_words, nc.scalar)
-        load_plane(shelves_plane, shelves_scales, [nc.sync, nc.scalar, nc.sync, nc.scalar])
-        slope_t = load_col("slope_t", slope, nc.sync)
+        load_plane(users_plane, users_scales, [nc.scalar, nc.sync, nc.scalar, nc.sync])
+        load_rows(keys_plane, keys_scales, 2, nc.gpsimd)
+        load_rows(keys_plane, keys_scales, 3, nc.gpsimd)
+        users_w = load_fp8("users_w", users_words, nc.scalar)
+        shelves_w = load_fp4("shelves_w", shelves_words, nc.sync)
+        load_plane(shelves_plane, shelves_scales, [nc.scalar, nc.sync, nc.scalar, nc.sync])
         load_rows(keys_plane, keys_scales, 0, nc.scalar)
         keys_w = load_fp8("keys_w", keys_words, nc.sync)
-        for r in range(1, 4):
-            load_rows(keys_plane, keys_scales, r, nc.sync)
+        load_rows(keys_plane, keys_scales, 1, nc.sync)
         l4 = load_list("l4", offs4)
         notes_w = load_fp4("notes_w", notes_words, nc.sync)
+        load_plane(notes_plane, notes_scales, [nc.sync] * 4)
         l1 = load_list("l1", offs)
-        l2 = load_list("l2", offs2)
         l5 = load_list("l5", offs5)
+        l2 = load_list("l2", offs2)
         l6 = load_list("l6", offs6)
 
         q_bf = sb.tile([P, P, PACK], BF16, name="q_bf", align_bytes=64)
@@ -140,53 +142,46 @@ def tile_attend_twolocks_four_kernel(
         def part(lst, h):
             return lst[:, h * (HALF // GROUP):(h + 1) * (HALF // GROUP)]
 
-        def new(name, h):
-            return sb.tile([P, HALF], F32, name="%s%d" % (name, h))
+        def new(name, tag):
+            return sb.tile([P, HALF], F32, name=name, tag=tag)
 
-        def gate(name, window, lst, h):
-            t = new(name, h)
+        def gate(t, window, lst, h):
             nc.scalar.activation(t[:], window[:].indirect(part(lst, h)), SIGMOID, bias=thr_t[:], scale=slope_t[:])
             return t
 
-        def fetch(name, window, lst, h):
-            t = new(name, h)
-            nc.scalar.activation(t[:], window[:].indirect(part(lst, h)), COPY)
+        def fetch(t, window, lst, h, sign=1.0):
+            nc.scalar.activation(t[:], window[:].indirect(part(lst, h)), COPY, scale=sign)
             return t
 
-        def neg_product(g, s, h):
-            t = new("nv", h)
-            nc.vector.scalar_tensor_tensor(t[:], g[:], -1.0, s[:], MULT, MULT)
-            return t
+        for window, banks in ((c_sb, c_ps), (d_sb, d_ps), (a_sb, a_ps), (b_sb, b_ps)):
+            for h in range(2):
+                nc.vector.tensor_copy(out=window[:, cols(h)], in_=banks[h][:])
 
-        nc.vector.tensor_copy(out=c_sb[:, cols(0)], in_=c_ps[0][:])
-        nc.vector.tensor_copy(out=c_sb[:, cols(1)], in_=c_ps[1][:])
-        s2_0 = gate("s2_", c_sb, l3, 0)
-        nc.vector.tensor_copy(out=d_sb[:, cols(0)], in_=d_ps[0][:])
-        nc.vector.tensor_copy(out=d_sb[:, cols(1)], in_=d_ps[1][:])
-        g4_0 = fetch("g4_", d_sb, l4, 0)
-        nc.vector.tensor_copy(out=a_sb[:, cols(0)], in_=a_ps[0][:])
-        nc.scalar.copy(out=a_sb[:, cols(1)], in_=a_ps[1][:])
-        s1_0 = gate("s1_", a_sb, l1, 0)
-        nv_0 = neg_product(g4_0, s2_0, 0)
-        nc.vector.tensor_copy(out=b_sb[:, cols(0)], in_=b_ps[0][:])
-        nc.vector.tensor_copy(out=b_sb[:, cols(1)], in_=b_ps[1][:])
-        w_0 = new("w", 0)
+        s2 = [gate(new("s2_%d" % h, "s2_%d" % h), c_sb, l3, h) for h in range(2)]
+        nv = []
+        for h in range(2):
+            g4 = fetch(new("g4_%d" % h, "g4_%d" % h), d_sb, l4, h, -1.0)
+            t = new("nv_%d" % h, "nv_%d" % h)
+            nc.gpsimd.tensor_tensor(t[:], g4[:], s2[h][:], MULT)
+            nv.append(t)
+
+        s1_0 = gate(new("s1_0", "s1"), a_sb, l1, 0)
+        w_0 = new("w_0", "w_0")
         nc.vector.tensor_tensor(w_0[:], b_sb[:].indirect(part(l2, 0)), s1_0[:], MULT)
-        nc.vector.tensor_tensor(f1[:].indirect(part(l5, 0)), w_0[:], nv_0[:], ADD)
+        nc.vector.tensor_tensor(f1[:].indirect(part(l5, 0)), w_0[:], nv[0][:], ADD)
 
-        s2_1 = gate("s2_", c_sb, l3, 1)
-        g4_1 = fetch("g4_", d_sb, l4, 1)
-        s1_1 = gate("s1_", a_sb, l1, 1)
-        g2_1 = fetch("g2_", b_sb, l2, 1)
-        nv_1 = neg_product(g4_1, s2_1, 1)
-        w_1 = new("w", 1)
+        g2_1 = fetch(new("g2_1", "g2_1"), b_sb, l2, 1)
+        s1_1 = gate(new("s1_1", "s1"), a_sb, l1, 1)
+        w_1 = new("w_1", "w_1")
         nc.vector.tensor_tensor(w_1[:], g2_1[:], s1_1[:], MULT)
-        nc.vector.tensor_tensor(f1[:].indirect(part(l5, 1)), w_1[:], nv_1[:], ADD)
+        nc.vector.tensor_tensor(f1[:].indirect(part(l5, 1)), w_1[:], nv[1][:], ADD)
 
         bb = sb.tile([P, COLS], F32, name="bb")
-        nc.vector.tensor_tensor(bb[:], b_sb[:], f1[:], ADD)
-        y_0 = new("y", 0)
+        nc.vector.tensor_tensor(bb[:, cols(0)], f1[:, cols(0)], b_ps[0][:], ADD)
+        nc.gpsimd.tensor_tensor(bb[:, SPLIT:COLS], f1[:, SPLIT:COLS], b_sb[:, SPLIT:COLS], ADD)
+        nc.vector.tensor_tensor(bb[:, BANK:SPLIT], f1[:, BANK:SPLIT], b_ps[1][:, 0:SPLIT - BANK], ADD)
+        y_0 = new("y_0", "y_0")
         nc.vector.tensor_copy(y_0[:], bb[:].indirect(part(l6, 0)))
         nc.sync.dma_start(out=out[:, 0:HALF], in_=y_0[:])
-        y_1 = fetch("y", bb, l6, 1)
+        y_1 = fetch(new("y_1", "y_1"), bb, l6, 1)
         nc.scalar.dma_start(out=out[:, HALF:SLOTS], in_=y_1[:])

@@ -79,13 +79,13 @@ def tile_attend_twolocks_four_kernel(
         l3 = load_list("l3", offs3)
         slope_t = load_col("slope_t", slope, nc.gpsimd)
         thr_t = load_col("thr_t", thr, nc.sync)
-        load_plane(users_plane, users_scales, [nc.scalar, nc.sync, nc.scalar, nc.sync])
+        load_plane(users_plane, users_scales, [nc.scalar, nc.scalar, nc.sync, nc.sync])
         load_rows(keys_plane, keys_scales, 2, nc.gpsimd)
         load_rows(keys_plane, keys_scales, 3, nc.gpsimd)
-        users_w = load_fp8("users_w", users_words, nc.scalar)
+        users_w = load_fp8("users_w", users_words, nc.sync)
         shelves_w = load_fp4("shelves_w", shelves_words, nc.sync)
-        load_plane(shelves_plane, shelves_scales, [nc.scalar, nc.sync, nc.scalar, nc.sync])
-        load_rows(keys_plane, keys_scales, 0, nc.scalar)
+        load_plane(shelves_plane, shelves_scales, [nc.sync] * 4)
+        load_rows(keys_plane, keys_scales, 0, nc.sync)
         keys_w = load_fp8("keys_w", keys_words, nc.sync)
         load_rows(keys_plane, keys_scales, 1, nc.sync)
         l4 = load_list("l4", offs4)
@@ -158,23 +158,22 @@ def tile_attend_twolocks_four_kernel(
                 nc.vector.tensor_copy(out=window[:, cols(h)], in_=banks[h][:])
 
         s2 = [gate(new("s2_%d" % h, "s2_%d" % h), c_sb, l3, h) for h in range(2)]
-        nv = []
-        for h in range(2):
-            g4 = fetch(new("g4_%d" % h, "g4_%d" % h), d_sb, l4, h, -1.0)
-            t = new("nv_%d" % h, "nv_%d" % h)
-            nc.gpsimd.tensor_tensor(t[:], g4[:], s2[h][:], MULT)
-            nv.append(t)
-
-        s1_0 = gate(new("s1_0", "s1"), a_sb, l1, 0)
-        w_0 = new("w_0", "w_0")
-        nc.vector.tensor_tensor(w_0[:], b_sb[:].indirect(part(l2, 0)), s1_0[:], MULT)
-        nc.vector.tensor_tensor(f1[:].indirect(part(l5, 0)), w_0[:], nv[0][:], ADD)
-
+        g4_0 = fetch(new("g4_0", "g4_0"), d_sb, l4, 0, -1.0)
+        nv_0 = new("nv_0", "nv_0")
+        nc.gpsimd.tensor_tensor(nv_0[:], g4_0[:], s2[0][:], MULT)
+        s1_0 = gate(new("s1_0", "factor"), a_sb, l1, 0)
+        s1_1 = gate(new("s1_1", "s1_1"), a_sb, l1, 1)
         g2_1 = fetch(new("g2_1", "g2_1"), b_sb, l2, 1)
-        s1_1 = gate(new("s1_1", "s1"), a_sb, l1, 1)
-        w_1 = new("w_1", "w_1")
+        w_0 = new("w_0", "w")
+        nc.vector.tensor_tensor(w_0[:], b_sb[:].indirect(part(l2, 0)), s1_0[:], MULT)
+        nc.vector.tensor_tensor(f1[:].indirect(part(l5, 0)), w_0[:], nv_0[:], ADD)
+
+        g4_1 = fetch(new("g4_1", "factor"), d_sb, l4, 1, -1.0)
+        nv_1 = new("nv_1", "nv_1")
+        nc.vector.tensor_tensor(nv_1[:], g4_1[:], s2[1][:], MULT)
+        w_1 = new("w_1", "w")
         nc.vector.tensor_tensor(w_1[:], g2_1[:], s1_1[:], MULT)
-        nc.vector.tensor_tensor(f1[:].indirect(part(l5, 1)), w_1[:], nv[1][:], ADD)
+        nc.vector.tensor_tensor(f1[:].indirect(part(l5, 1)), w_1[:], nv_1[:], ADD)
 
         bb = sb.tile([P, COLS], F32, name="bb")
         nc.vector.tensor_tensor(bb[:, cols(0)], f1[:, cols(0)], b_ps[0][:], ADD)

from contextlib import ExitStack

import concourse.mybir as mybir

F32 = mybir.dt.float32
BF16 = mybir.dt.bfloat16
I32 = mybir.dt.int32
U32 = mybir.dt.uint32
U16 = mybir.dt.uint16
U8 = mybir.dt.uint8
FP8X4 = mybir.dt.float8_e4m3fn_x4
FP4X4 = mybir.dt.float4_e2m1fn_x4
MULT = mybir.AluOpType.mult
ADD = mybir.AluOpType.add
SIGMOID = mybir.ActivationFunctionType.Sigmoid
COPY = mybir.ActivationFunctionType.Copy

P = 128
PACK = 4
COLS = 1024
BANK = 512
SLOTS = 512
HALF = SLOTS // 2
GROUP = 16
SPLIT = 720

FLOPS = 2 * 512 * 128 * 4 * 1024


def tile_attend_twolocks_four_kernel(
    tc, query, keys_words, keys_scales, notes_words, notes_scales, users_words, users_scales,
    shelves_words, shelves_scales, thr, slope, offs, offs2, offs3, offs4, offs5, offs6, out,
):
    nc = tc.nc
    with ExitStack() as ctx:
        sb = ctx.enter_context(tc.tile_pool(name="sb", bufs=1))
        ps = ctx.enter_context(tc.psum_pool(name="ps", bufs=1))

        def plane(name):
            t = sb.tile([P, COLS], U8, name=name, align_bytes=64)
            nc.vector.memset(t[:].bitcast(I32), 0)
            return t

        def load_rows(t, scales, r, queue):
            rows = scales[0].bitcast(I32)
            queue.dma_start(out=t[r:P:32, :].bitcast(I32), in_=rows[r:16:4, :])

        def load_plane(t, scales, queues):
            for r in range(4):
                load_rows(t, scales, r, queues[r])

        def load_list(name, src):
            t = sb.tile([P, SLOTS // GROUP], U16, name=name)
            nc.sync.dma_start(t[:], src)
            return t

        def load_fp8(name, words, queue):
            t = sb.tile([P, COLS], U32, name=name, align_bytes=64)
            queue.dma_start(out=t[:].bitcast(I32), in_=words[0].rearrange("p n t -> p (n t)").bitcast(I32))
            return t

        def load_fp4(name, words, queue):
            t = sb.tile([P, 2 * COLS], U8, name=name, align_bytes=64)
            queue.dma_start(out=t[:].bitcast(I32), in_=words[0].bitcast(I32))
            return t

        def load_col(name, src, queue):
            t = sb.tile([P, 1], F32, name=name)
            queue.dma_start(out=t[:], in_=src)
            return t

        users_plane = plane("users_plane")
        keys_plane = plane("keys_plane")
        shelves_plane = plane("shelves_plane")
        notes_plane = plane("notes_plane")

        q_raw = sb.tile([P, PACK, P], F32, name="q_raw")
        nc.scalar.dma_start(out=q_raw[:], in_=query.rearrange("(p j) q -> p j q", j=PACK))
        l3 = load_list("l3", offs3)
        slope_t = load_col("slope_t", slope, nc.gpsimd)
        thr_t = load_col("thr_t", thr, nc.sync)
        load_plane(users_plane, users_scales, [nc.scalar, nc.scalar, nc.sync, nc.sync])
        load_rows(keys_plane, keys_scales, 2, nc.gpsimd)
        load_rows(keys_plane, keys_scales, 3, nc.gpsimd)
        users_w = load_fp8("users_w", users_words, nc.sync)
        shelves_w = load_fp4("shelves_w", shelves_words, nc.sync)
        load_plane(shelves_plane, shelves_scales, [nc.sync] * 4)
        load_rows(keys_plane, keys_scales, 0, nc.sync)
        keys_w = load_fp8("keys_w", keys_words, nc.sync)
        load_rows(keys_plane, keys_scales, 1, nc.sync)
        l4 = load_list("l4", offs4)
        notes_w = load_fp4("notes_w", notes_words, nc.sync)
        load_plane(notes_plane, notes_scales, [nc.sync] * 4)
        l1 = load_list("l1", offs)
        l5 = load_list("l5", offs5)
        l2 = load_list("l2", offs2)
        l6 = load_list("l6", offs6)

        q_bf = sb.tile([P, P, PACK], BF16, name="q_bf", align_bytes=64)
        nc.vector.tensor_copy(
            out=q_bf[:].rearrange("p (c i) t -> p c t i", i=4),
            in_=q_raw[:].rearrange("p t (c i) -> p c t i", i=4),
        )
        q_codes = sb.tile([P, P], U32, name="q_codes", align_bytes=64)
        q_plane = sb.tile([P, P], U8, name="q_plane", align_bytes=64)
        nc.vector.quantize_mx(
            out=q_codes[:].bitcast(FP8X4), scales=q_plane[:], in_=q_bf[:].rearrange("p c t -> p (c t)")
        )
        f1 = sb.tile([P, COLS], F32, name="f1")
        nc.vector.memset(f1[:], 0.0)

        def scores(name, moving, scale_plane):
            banks = []
            for h in range(2):
                bank = ps.tile([P, BANK], F32, name="%s_bank%d" % (name, h))
                nc.tensor.matmul_mx(
                    out=bank[:], lhsT=q_codes[:].bitcast(FP8X4), lhsT_scale=q_plane[:],
                    rhs=moving[h], rhs_scale=scale_plane[:, h * BANK:(h + 1) * BANK], start=True, stop=True,
                )
                banks.append(bank)
            return banks

        def fp4_halves(t):
            return [t[:, h * 2 * BANK:(h + 1) * 2 * BANK].bitcast(FP4X4) for h in range(2)]

        def fp8_halves(t):
            return [t[:, h * BANK:(h + 1) * BANK].bitcast(FP8X4) for h in range(2)]

        c_ps = scores("c", fp8_halves(users_w), users_plane)
        d_ps = scores("d", fp4_halves(shelves_w), shelves_plane)
        a_ps = scores("a", fp8_halves(keys_w), keys_plane)
        b_ps = scores("b", fp4_halves(notes_w), notes_plane)

        a_sb = sb.tile([P, COLS], F32, name="a_sb")
        b_sb = sb.tile([P, COLS], F32, name="b_sb")
        c_sb = sb.tile([P, COLS], F32, name="c_sb")
        d_sb = sb.tile([P, COLS], F32, name="d_sb")

        def cols(h):
            return slice(h * BANK, (h + 1) * BANK)

        def part(lst, h):
            return lst[:, h * (HALF // GROUP):(h + 1) * (HALF // GROUP)]

        def new(name, tag):
            return sb.tile([P, HALF], F32, name=name, tag=tag)

        def gate(t, window, lst, h):
            nc.scalar.activation(t[:], window[:].indirect(part(lst, h)), SIGMOID, bias=thr_t[:], scale=slope_t[:])
            return t

        def fetch(t, window, lst, h, sign=1.0):
            nc.scalar.activation(t[:], window[:].indirect(part(lst, h)), COPY, scale=sign)
            return t

        for window, banks in ((c_sb, c_ps), (d_sb, d_ps), (a_sb, a_ps), (b_sb, b_ps)):
            for h in range(2):
                nc.vector.tensor_copy(out=window[:, cols(h)], in_=banks[h][:])

        s2 = [gate(new("s2_%d" % h, "s2_%d" % h), c_sb, l3, h) for h in range(2)]
        g4_0 = fetch(new("g4_0", "g4_0"), d_sb, l4, 0, -1.0)
        nv_0 = new("nv_0", "nv_0")
        nc.gpsimd.tensor_tensor(nv_0[:], g4_0[:], s2[0][:], MULT)
        s1_0 = gate(new("s1_0", "factor"), a_sb, l1, 0)
        s1_1 = gate(new("s1_1", "s1_1"), a_sb, l1, 1)
        g2_1 = fetch(new("g2_1", "g2_1"), b_sb, l2, 1)
        w_0 = new("w_0", "w")
        nc.vector.tensor_tensor(w_0[:], b_sb[:].indirect(part(l2, 0)), s1_0[:], MULT)
        nc.vector.tensor_tensor(f1[:].indirect(part(l5, 0)), w_0[:], nv_0[:], ADD)

        g4_1 = fetch(new("g4_1", "factor"), d_sb, l4, 1, -1.0)
        nv_1 = new("nv_1", "nv_1")
        nc.vector.tensor_tensor(nv_1[:], g4_1[:], s2[1][:], MULT)
        w_1 = new("w_1", "w")
        nc.vector.tensor_tensor(w_1[:], g2_1[:], s1_1[:], MULT)
        nc.vector.tensor_tensor(f1[:].indirect(part(l5, 1)), w_1[:], nv_1[:], ADD)

        bb = sb.tile([P, COLS], F32, name="bb")
        nc.vector.tensor_tensor(bb[:, cols(0)], f1[:, cols(0)], b_ps[0][:], ADD)
        nc.gpsimd.tensor_tensor(bb[:, SPLIT:COLS], f1[:, SPLIT:COLS], b_sb[:, SPLIT:COLS], ADD)
        nc.vector.tensor_tensor(bb[:, BANK:SPLIT], f1[:, BANK:SPLIT], b_ps[1][:, 0:SPLIT - BANK], ADD)
        y_0 = new("y_0", "y_0")
        nc.vector.tensor_copy(y_0[:], bb[:].indirect(part(l6, 0)))
        nc.sync.dma_start(out=out[:, 0:HALF], in_=y_0[:])
        y_1 = fetch(new("y_1", "y_1"), bb, l6, 1)
        nc.scalar.dma_start(out=out[:, HALF:SLOTS], in_=y_1[:])
